import numpy as np
import ml_dtypes


def mxq(x, axis, fmt="e4m3"):
    dtype, down = {"e4m3": (ml_dtypes.float8_e4m3fn, 7), "e5m2": (ml_dtypes.float8_e5m2, 14)}[fmt]
    v = np.moveaxis(np.asarray(x, np.float32).astype(ml_dtypes.bfloat16).astype(np.float64), axis, -1)
    blocks = v.reshape(v.shape[:-1] + (-1, 32))
    amax = np.abs(blocks).max(-1, keepdims=True)
    byte = np.maximum(np.where(amax > 0, np.frexp(amax)[1] - 1 + 127, 0) - down, 1)
    scale = np.exp2(byte - 127.0)
    codes = (blocks / scale).astype(np.float32).astype(dtype).astype(np.float64)
    return np.moveaxis((codes * scale).reshape(v.shape), -1, axis)


WIDE = False


def mx_kscale(k):
    if not WIDE:
        return np.ones(k)
    levels = np.array([10, -10, 5, -5, 0])
    if k % 512:
        return np.exp2(np.random.permutation(np.resize(levels, k // 32))).repeat(32)
    a = np.empty((k // 512, 16))
    for p in range(k // 512):
        a[p, :8] = np.random.permutation(np.resize(levels, 8))
        for g in range(8):
            far = levels[np.abs(levels - a[p, g]) >= 10]
            a[p, g + 8] = far[np.random.randint(len(far))]
    return np.exp2(a.ravel()).repeat(32)


def f64(x):
    return np.asarray(x).astype(np.float64)


def striped(idx):
    return np.tile(idx.reshape(-1, 16).T, (8, 1)).astype(np.uint16)


def unstriped(offs):
    return offs[:16].T.reshape(-1).astype(np.int64)


def striped8(idx):
    return np.concatenate([x.reshape(-1, 16).T for x in idx]).astype(np.uint16)


def runs(offs, k):
    lists = np.stack([offs[16 * r : 16 * r + 16].T.reshape(-1) for r in range(8)]).astype(np.int64)
    return lists[np.arange(k) % 512 // 64]


def pack_weight(w):
    k, n = w.shape
    w = f64(np.asarray(w, np.float32).astype(ml_dtypes.bfloat16)).reshape(k // 32, 32, n)
    amax = np.abs(w).max(1)
    byte = np.clip(np.where(amax > 0, np.frexp(amax)[1] - 1 + 127 - 7, 1), 1, 254)
    scaled = (w * np.exp2(127.0 - byte)[:, None, :]).reshape(k, n).astype(np.float32)
    words = np.ascontiguousarray(scaled.reshape(k // 512, 128, 4, n).transpose(0, 1, 3, 2)).astype(ml_dtypes.float8_e4m3fn).view(np.uint8)
    return words, np.ascontiguousarray(byte.astype(np.uint8).reshape(k // 512, 16, n))


def unpack_weight(words, scales):
    g, p, n, _ = words.shape
    vals = np.ascontiguousarray(words).view(ml_dtypes.float8_e4m3fn).astype(np.float64) * np.repeat(np.exp2(scales.astype(np.float64) - 127.0), 8, axis=1)[..., None]
    return vals.transpose(0, 1, 3, 2).reshape(g * 512, n)


def sigmoid(v):
    return 1.0 / (1.0 + np.exp(-np.maximum(v, -700.0)))


K, T, S, N, H = 512, 2048, 512, 512, 512


def setup_inputs():
    n = np.random.standard_normal
    s = mx_kscale(K)[:, None]
    u = mx_kscale(H)
    packed_xT = pack_weight(n((K, T)) * s)
    return {
        "x_words": packed_xT[0],
        "x_scales": packed_xT[1],
        "w1": (n((K, H)) / np.sqrt(K) / s).astype(np.float32),
        "gn": (np.random.uniform(0.5, 1.5, (H, 1)) * u[:, None]).astype(np.float32),
        "w2": (n((H, N)) / np.sqrt(H) / u[:, None]).astype(np.float32),
        "offs": striped(np.random.permutation(T)[:S]),
        "n1": striped8(np.stack([np.random.permutation(S) for _ in range(8)])),
        "n2": striped8(np.stack([np.random.permutation(S) for _ in range(8)])),
        "n3": striped8(np.stack([np.random.permutation(S) for _ in range(8)])),
    }


def reference(x_words, x_scales, w1, gn, w2, offs, n1, n2, n3):
    xq = unpack_weight(x_words, x_scales)[:, unstriped(offs)]
    y = mxq(f64(w1), 0, "e4m3").T @ xq
    z = f64(gn) * (0.75 * ((y - (y[np.arange(H)[:, None], runs(n1, H)])) * (y - (y[np.arange(H)[:, None], runs(n2, H)]))))
    h = mxq(f64(w2), 0, "e4m3").T @ mxq(z, 0, "e4m3")
    st = h * (sigmoid(h[np.arange(N)[:, None], runs(n3, N)]))
    return np.maximum(st, st[np.arange(N)[:, None], runs(n3, N)])

@@ -1,0 +1,195 @@
+from contextlib import ExitStack
+
+import concourse.mybir as mybir
+
+K, T, S, N, H = 512, 2048, 512, 512, 512
+FLOPS = 2 * K * H * S + 2 * H * N * S
+
+F32 = mybir.dt.float32
+BF16 = mybir.dt.bfloat16
+I32 = mybir.dt.int32
+U32 = mybir.dt.uint32
+U16 = mybir.dt.uint16
+U8 = mybir.dt.uint8
+FP8X4 = mybir.dt.float8_e4m3fn_x4
+ALU = mybir.AluOpType
+ACT = mybir.ActivationFunctionType
+
+P = 128
+PACK = 4
+HALF = S // 2
+LIST_ROWS = 16
+
+
+def tile_picked_layquadtwicp_none_p_kernel(tc, x_words, x_scales, w1, gn, w2, offs, n1, n2, n3, out):
+    nc = tc.nc
+    halves = [slice(0, HALF), slice(HALF, S)]
+    list_halves = [slice(0, HALF // LIST_ROWS), slice(HALF // LIST_ROWS, S // LIST_ROWS)]
+
+    with ExitStack() as ctx:
+        keep = ctx.enter_context(tc.tile_pool(name="keep", bufs=1))
+        psum = ctx.enter_context(tc.psum_pool(name="psum", bufs=1))
+
+        def sb(name, shape, dtype):
+            return keep.tile(shape, dtype, name=name, align_bytes=64)
+
+        def bank(b, name):
+            return psum.tile([P, S], F32, name=name, tag="bank%d" % b)
+
+        offs_t = sb("offs_t", [P, S // LIST_ROWS], U16)
+        n1_t = sb("n1_t", [P, S // LIST_ROWS], U16)
+        n2_t = sb("n2_t", [P, S // LIST_ROWS], U16)
+        n3_t = sb("n3_t", [P, S // LIST_ROWS], U16)
+        x_table = sb("x_table", [P, T], U32)
+        s_table = sb("s_table", [P, T], U8)
+        w1_raw = sb("w1_raw", [P, PACK, H], F32)
+        w2_raw = sb("w2_raw", [P, PACK, N], F32)
+        gain_raw = sb("gain_raw", [P, PACK], F32)
+        gain = sb("gain", [P, PACK], F32)
+        warm_in = sb("warm_in", [P, 1], F32)
+        warm_out = sb("warm_out", [P, 1], F32)
+
+        nc.vector.memset(s_table[:].bitcast(I32), 0)
+        nc.vector.memset(warm_in[:], 0.0)
+        nc.scalar.activation(out=warm_out[:], in_=warm_in[:], func=ACT.Sigmoid)
+
+        nc.sync.dma_start(w1_raw[:], w1.rearrange("(p j) c -> p j c", j=PACK))
+        nc.sync.dma_start(offs_t[:], offs)
+        for q in range(4):
+            nc.sync.dma_start(s_table[32 * q : 32 * q + 4, :].bitcast(I32), x_scales[0, 4 * q : 4 * q + 4, :].bitcast(I32))
+        nc.sync.dma_start(x_table[:].bitcast(I32), x_words[0].rearrange("p n t -> p (n t)").bitcast(I32))
+        nc.sync.dma_start(n1_t[:], n1)
+        nc.sync.dma_start(n2_t[:], n2)
+        nc.sync.dma_start(gain_raw[:], gn.rearrange("(p t) o -> p (t o)", t=PACK))
+        nc.sync.dma_start(w2_raw[:], w2.rearrange("(p j) c -> p j c", j=PACK))
+        nc.sync.dma_start(n3_t[:], n3)
+
+        nc.gpsimd.tensor_scalar(out=gain[:], in0=gain_raw[:], scalar1=0.75, scalar2=0.0, op0=ALU.mult, op1=ALU.add)
+
+        x_codes = sb("x_codes", [P, S], U32)
+        x_scale = sb("x_scale", [P, S], U8)
+
+        def deal(copy, raw, pair, name):
+            grouped = sb(name, [P, 2, P, PACK], BF16)
+            copy(
+                out=grouped[:].rearrange("p e m j -> p m j e"),
+                in_=raw[:].rearrange("p j (m u e) -> p u m j e", u=2, e=2)[:, pair],
+            )
+            return grouped
+
+        def quantize(flat, width, name):
+            codes = sb(name + "_codes", [P, width], U32)
+            scale = sb(name + "_scale", [P, width], U8)
+            nc.vector.quantize_mx(out=codes[:].bitcast(FP8X4), scales=scale[:], in_=flat)
+            return codes, scale
+
+        def product(acc, stationary, m_cols, moving, n_cols):
+            nc.tensor.matmul_mx(
+                out=acc,
+                lhsT=stationary[0][:, m_cols].bitcast(FP8X4),
+                lhsT_scale=stationary[1][:, m_cols],
+                rhs=moving[0][:, n_cols].bitcast(FP8X4),
+                rhs_scale=moving[1][:, n_cols],
+                start=True,
+                stop=True,
+            )
+
+        every = slice(0, P)
+        w1_lo = deal(nc.vector.tensor_copy, w1_raw, 0, "w1_lo")
+        w1_hi = deal(nc.scalar.copy, w1_raw, 1, "w1_hi")
+        w1_q = [quantize(w1_lo[:, e].rearrange("p m j -> p (m j)"), P, "w1_q%d" % e) for e in range(2)]
+        w1_q_hi = quantize(w1_hi[:].rearrange("p e m j -> p (e m j)"), 2 * P, "w1_q_hi")
+        w1_ops = [(w1_q[0], every), (w1_q[1], every), (w1_q_hi, slice(0, P)), (w1_q_hi, slice(P, 2 * P))]
+        x_q = (x_codes, x_scale)
+        nc.vector.tensor_copy(out=x_scale[:], in_=s_table[:].indirect(offs_t[:]))
+        for c in range(2):
+            nc.vector.tensor_copy(out=x_codes[:, halves[c]], in_=x_table[:].indirect(offs_t[:, list_halves[c]]))
+
+        y_win = [sb("y_win%d" % t, [P, S], F32) for t in range(PACK)]
+        y_own = [sb("y_own%d" % t, [P, S], F32) for t in range(PACK)]
+        for c, copy in enumerate((nc.scalar.copy, nc.vector.tensor_copy)):
+            acc = bank(c, "y0_%d" % c)
+            product(acc[:, 0:HALF], w1_ops[0][0], w1_ops[0][1], x_q, halves[c])
+            copy(out=y_win[0][:, halves[c]], in_=acc[:, 0:HALF])
+            nc.scalar.copy(out=y_own[0][:, halves[c]], in_=acc[:, 0:HALF])
+        for t in range(1, PACK):
+            acc = bank(1 + t, "y%d" % t)
+            product(acc[:], w1_ops[t][0], w1_ops[t][1], x_q, slice(0, S))
+            nc.scalar.copy(out=y_win[t][:], in_=acc[:])
+            nc.scalar.copy(out=y_own[t][:], in_=acc[:])
+
+        d1 = [sb("d1_%d" % t, [P, S], F32) for t in range(PACK)]
+        d1g = [sb("d1g_%d" % c, [P, PACK, HALF], F32) for c in range(2)]
+        d2 = [sb("d2_%d" % c, [P, PACK, HALF], F32) for c in range(2)]
+
+        def difference(dst, t, lists, c):
+            nc.vector.tensor_tensor(out=dst, in0=y_win[t][:].indirect(lists[:, list_halves[c]]), in1=y_own[t][:, halves[c]], op=ALU.subtract)
+
+        def first_difference(t):
+            for c in range(2):
+                difference(d1[t][:, halves[c]], t, n1_t, c)
+                nc.scalar.activation(out=d1g[c][:, t, :], in_=d1[t][:, halves[c]], func=ACT.Copy, scale=gain[:, t : t + 1])
+
+        def hidden(c):
+            z = sb("z%d" % c, [P, HALF, PACK], BF16)
+            nc.vector.tensor_tensor(
+                out=z[:].rearrange("p (a i) t -> p a t i", i=2),
+                in0=d1g[c][:].rearrange("p t (a i) -> p a t i", i=2),
+                in1=d2[c][:].rearrange("p t (a i) -> p a t i", i=2),
+                op=ALU.mult,
+            )
+            return z[:].rearrange("p j t -> p (j t)")
+
+        for t in range(PACK - 1):
+            first_difference(t)
+            for c in range(2):
+                difference(d2[c][:, t, :], t, n2_t, c)
+        last = PACK - 1
+        first_difference(last)
+        w2_lo = deal(nc.scalar.copy, w2_raw, 0, "w2_lo")
+        w2_hi = deal(nc.scalar.copy, w2_raw, 1, "w2_hi")
+        difference(d2[0][:, last, :], last, n2_t, 0)
+        w2_q_lo = quantize(w2_lo[:].rearrange("p e m j -> p (e m j)"), 2 * P, "w2_q_lo")
+        z0 = hidden(0)
+        difference(d2[1][:, last, :], last, n2_t, 1)
+        z_q = [quantize(z0, HALF, "z_q0")]
+        z1 = hidden(1)
+        z_q.append(quantize(z1, HALF, "z_q1"))
+        w2_q_hi = quantize(w2_hi[:].rearrange("p e m j -> p (e m j)"), 2 * P, "w2_q_hi")
+        w2_ops = [(w2_q_lo, slice(0, P)), (w2_q_lo, slice(P, 2 * P)), (w2_q_hi, slice(0, P)), (w2_q_hi, slice(P, 2 * P))]
+
+        h_sb = [sb("h%d" % t, [P, S], F32) for t in range(PACK)]
+        gate = [sb("gate%d" % t, [P, S], F32) for t in range(PACK)]
+        h_acc = [bank((5 + t) % 8, "h_acc%d" % t) for t in range(PACK)]
+        for c in range(2):
+            for t in range(2):
+                product(h_acc[t][:, halves[c]], w2_ops[t][0], w2_ops[t][1], z_q[c], slice(0, HALF))
+                if t == 0:
+                    nc.scalar.activation(out=gate[0][:, halves[c]], in_=h_acc[0][:, halves[c]], func=ACT.Sigmoid)
+                nc.scalar.copy(out=h_sb[t][:, halves[c]], in_=h_acc[t][:, halves[c]])
+        for t in range(2, PACK):
+            for c in range(2):
+                product(h_acc[t][:, halves[c]], w2_ops[t][0], w2_ops[t][1], z_q[c], slice(0, HALF))
+
+        def gates(t):
+            if t >= 2:
+                nc.scalar.copy(out=h_sb[t][:], in_=h_acc[t][:])
+            for c in range(2):
+                nc.scalar.activation(out=gate[t][:, halves[c]], in_=h_sb[t][:].indirect(n3_t[:, list_halves[c]]), func=ACT.Sigmoid)
+
+        st = [sb("st%d" % t, [P, S], F32) for t in range(PACK)]
+        far = [sb("far%d" % t, [P, S], F32) for t in range(PACK)]
+        res = [sb("res%d" % t, [P, S], F32) for t in range(PACK)]
+        out_rows = out.rearrange("(p t) c -> p t c", t=PACK)
+
+        for c in range(2):
+            nc.vector.tensor_tensor(out=st[0][:, halves[c]], in0=gate[0][:].indirect(n3_t[:, list_halves[c]]), in1=h_sb[0][:, halves[c]], op=ALU.mult)
+        for t in range(PACK):
+            for c in range(2):
+                nc.vector.tensor_copy(out=far[t][:, halves[c]], in_=st[t][:].indirect(n3_t[:, list_halves[c]]))
+            if t < last:
+                gates(t + 1)
+                nc.vector.tensor_tensor(out=st[t + 1][:], in0=h_sb[t + 1][:], in1=gate[t + 1][:], op=ALU.mult)
+            for cols in ([slice(0, S)] if t < last else halves):
+                nc.vector.tensor_tensor(out=res[t][:, cols], in0=st[t][:, cols], in1=far[t][:, cols], op=ALU.max)
+                nc.sync.dma_start(out_rows[:, t, cols], res[t][:, cols])

@@ -53,11 +53,11 @@ def tile_picked_layquadtwicp_none_p_kernel(tc, x_words, x_scales, w1, gn, w2, of
         nc.vector.memset(warm_in[:], 0.0)
         nc.scalar.activation(out=warm_out[:], in_=warm_in[:], func=ACT.Sigmoid)
 
-        nc.sync.dma_start(w1_raw[:], w1.rearrange("(p j) c -> p j c", j=PACK))
+        nc.sync.dma_start(x_table[:].bitcast(I32), x_words[0].rearrange("p n t -> p (n t)").bitcast(I32))
         nc.sync.dma_start(offs_t[:], offs)
         for q in range(4):
             nc.sync.dma_start(s_table[32 * q : 32 * q + 4, :].bitcast(I32), x_scales[0, 4 * q : 4 * q + 4, :].bitcast(I32))
-        nc.sync.dma_start(x_table[:].bitcast(I32), x_words[0].rearrange("p n t -> p (n t)").bitcast(I32))
+        nc.sync.dma_start(w1_raw[:], w1.rearrange("(p j) c -> p j c", j=PACK))
         nc.sync.dma_start(n1_t[:], n1)
         nc.sync.dma_start(n2_t[:], n2)
         nc.sync.dma_start(gain_raw[:], gn.rearrange("(p t) o -> p (t o)", t=PACK))
@@ -68,6 +68,8 @@ def tile_picked_layquadtwicp_none_p_kernel(tc, x_words, x_scales, w1, gn, w2, of
 
         x_codes = sb("x_codes", [P, S], U32)
         x_scale = sb("x_scale", [P, S], U8)
+        nc.vector.tensor_copy(out=x_codes[:], in_=x_table[:].indirect(offs_t[:]))
+        nc.vector.tensor_copy(out=x_scale[:], in_=s_table[:].indirect(offs_t[:]))
 
         def deal(copy, raw, pair, name):
             grouped = sb(name, [P, 2, P, PACK], BF16)
@@ -101,12 +103,10 @@ def tile_picked_layquadtwicp_none_p_kernel(tc, x_words, x_scales, w1, gn, w2, of
         w1_q_hi = quantize(w1_hi[:].rearrange("p e m j -> p (e m j)"), 2 * P, "w1_q_hi")
         w1_ops = [(w1_q[0], every), (w1_q[1], every), (w1_q_hi, slice(0, P)), (w1_q_hi, slice(P, 2 * P))]
         x_q = (x_codes, x_scale)
-        nc.vector.tensor_copy(out=x_scale[:], in_=s_table[:].indirect(offs_t[:]))
-        for c in range(2):
-            nc.vector.tensor_copy(out=x_codes[:, halves[c]], in_=x_table[:].indirect(offs_t[:, list_halves[c]]))
 
-        y_win = [sb("y_win%d" % t, [P, S], F32) for t in range(PACK)]
-        y_own = [sb("y_own%d" % t, [P, S], F32) for t in range(PACK)]
+        y_win = [sb("y_win%d" % t, [P, S if t == 0 else 2 * S], F32) for t in range(PACK)]
+        y_last = sb("y_last", [P, S], F32)
+        y_own = [y_win[t + 1][:, S : 2 * S] for t in range(PACK - 1)] + [y_last[:]]
         for c, copy in enumerate((nc.scalar.copy, nc.vector.tensor_copy)):
             acc = bank(c, "y0_%d" % c)
             product(acc[:, 0:HALF], w1_ops[0][0], w1_ops[0][1], x_q, halves[c])
@@ -115,50 +115,52 @@ def tile_picked_layquadtwicp_none_p_kernel(tc, x_words, x_scales, w1, gn, w2, of
         for t in range(1, PACK):
             acc = bank(1 + t, "y%d" % t)
             product(acc[:], w1_ops[t][0], w1_ops[t][1], x_q, slice(0, S))
-            nc.scalar.copy(out=y_win[t][:], in_=acc[:])
-            nc.scalar.copy(out=y_own[t][:], in_=acc[:])
+            nc.scalar.copy(out=y_win[t][:, 0:S], in_=acc[:])
+            nc.scalar.copy(out=y_own[t], in_=acc[:])
 
         d1 = [sb("d1_%d" % t, [P, S], F32) for t in range(PACK)]
-        d1g = [sb("d1g_%d" % c, [P, PACK, HALF], F32) for c in range(2)]
-        d2 = [sb("d2_%d" % c, [P, PACK, HALF], F32) for c in range(2)]
+        d1g = sb("d1g", [P, PACK, S], F32)
+        d2 = sb("d2", [P, PACK, S], F32)
+        last = PACK - 1
+        whole = slice(0, S)
 
-        def difference(dst, t, lists, c):
-            nc.vector.tensor_tensor(out=dst, in0=y_win[t][:].indirect(lists[:, list_halves[c]]), in1=y_own[t][:, halves[c]], op=ALU.subtract)
+        def entries(lists, cols):
+            return lists[:, cols.start // LIST_ROWS : cols.stop // LIST_ROWS]
 
-        def first_difference(t):
-            for c in range(2):
-                difference(d1[t][:, halves[c]], t, n1_t, c)
-                nc.scalar.activation(out=d1g[c][:, t, :], in_=d1[t][:, halves[c]], func=ACT.Copy, scale=gain[:, t : t + 1])
+        def difference(dst, t, lists, cols):
+            nc.vector.tensor_tensor(out=dst[:, cols], in0=y_win[t][:].indirect(entries(lists, cols)), in1=y_own[t][:, cols], op=ALU.subtract)
 
         def hidden(c):
             z = sb("z%d" % c, [P, HALF, PACK], BF16)
             nc.vector.tensor_tensor(
                 out=z[:].rearrange("p (a i) t -> p a t i", i=2),
-                in0=d1g[c][:].rearrange("p t (a i) -> p a t i", i=2),
-                in1=d2[c][:].rearrange("p t (a i) -> p a t i", i=2),
+                in0=d1g[:, :, halves[c]].rearrange("p t (a i) -> p a t i", i=2),
+                in1=d2[:, :, halves[c]].rearrange("p t (a i) -> p a t i", i=2),
                 op=ALU.mult,
             )
             return z[:].rearrange("p j t -> p (j t)")
 
-        for t in range(PACK - 1):
-            first_difference(t)
-            for c in range(2):
-                difference(d2[c][:, t, :], t, n2_t, c)
-        last = PACK - 1
-        first_difference(last)
+        for t in range(PACK):
+            for cols in (halves if t == 0 else [whole]):
+                difference(d1[t], t, n1_t, cols)
+            nc.scalar.activation(out=d1g[:, t, :], in_=d1[t][:], func=ACT.Copy, scale=gain[:, t : t + 1])
+            if t < last:
+                for cols in (halves if t == 0 else [whole]):
+                    difference(d2[:, t, :], t, n2_t, cols)
         w2_lo = deal(nc.scalar.copy, w2_raw, 0, "w2_lo")
         w2_hi = deal(nc.scalar.copy, w2_raw, 1, "w2_hi")
-        difference(d2[0][:, last, :], last, n2_t, 0)
+        difference(d2[:, last, :], last, n2_t, halves[0])
         w2_q_lo = quantize(w2_lo[:].rearrange("p e m j -> p (e m j)"), 2 * P, "w2_q_lo")
         z0 = hidden(0)
-        difference(d2[1][:, last, :], last, n2_t, 1)
+        difference(d2[:, last, :], last, n2_t, halves[1])
         z_q = [quantize(z0, HALF, "z_q0")]
         z1 = hidden(1)
         z_q.append(quantize(z1, HALF, "z_q1"))
         w2_q_hi = quantize(w2_hi[:].rearrange("p e m j -> p (e m j)"), 2 * P, "w2_q_hi")
         w2_ops = [(w2_q_lo, slice(0, P)), (w2_q_lo, slice(P, 2 * P)), (w2_q_hi, slice(0, P)), (w2_q_hi, slice(P, 2 * P))]
 
-        h_sb = [sb("h%d" % t, [P, S], F32) for t in range(PACK)]
+        st_win = [sb("st_win%d" % t, [P, 2 * S], F32) for t in range(PACK)]
+        h_sb = [st_win[0][:, S : 2 * S]] + [sb("h%d" % t, [P, S], F32)[:] for t in range(1, PACK)]
         gate = [sb("gate%d" % t, [P, S], F32) for t in range(PACK)]
         h_acc = [bank((5 + t) % 8, "h_acc%d" % t) for t in range(PACK)]
         for c in range(2):
@@ -173,23 +175,23 @@ def tile_picked_layquadtwicp_none_p_kernel(tc, x_words, x_scales, w1, gn, w2, of
 
         def gates(t):
             if t >= 2:
-                nc.scalar.copy(out=h_sb[t][:], in_=h_acc[t][:])
+                nc.scalar.copy(out=h_sb[t], in_=h_acc[t][:])
             for c in range(2):
-                nc.scalar.activation(out=gate[t][:, halves[c]], in_=h_sb[t][:].indirect(n3_t[:, list_halves[c]]), func=ACT.Sigmoid)
+                nc.scalar.activation(out=gate[t][:, halves[c]], in_=h_sb[t].indirect(n3_t[:, list_halves[c]]), func=ACT.Sigmoid)
 
-        st = [sb("st%d" % t, [P, S], F32) for t in range(PACK)]
-        far = [sb("far%d" % t, [P, S], F32) for t in range(PACK)]
+        st = [st_win[t][:, 0:S] for t in range(PACK)]
+        far = [st_win[t + 1][:, S : 2 * S] for t in range(PACK - 1)] + [sb("far_last", [P, S], F32)[:]]
         res = [sb("res%d" % t, [P, S], F32) for t in range(PACK)]
         out_rows = out.rearrange("(p t) c -> p t c", t=PACK)
 
         for c in range(2):
             nc.vector.tensor_tensor(out=st[0][:, halves[c]], in0=gate[0][:].indirect(n3_t[:, list_halves[c]]), in1=h_sb[0][:, halves[c]], op=ALU.mult)
         for t in range(PACK):
-            for c in range(2):
-                nc.vector.tensor_copy(out=far[t][:, halves[c]], in_=st[t][:].indirect(n3_t[:, list_halves[c]]))
+            for cols in ([whole] if t < last else halves):
+                nc.vector.tensor_copy(out=far[t][:, cols], in_=st_win[t][:].indirect(entries(n3_t, cols)))
             if t < last:
                 gates(t + 1)
-                nc.vector.tensor_tensor(out=st[t + 1][:], in0=h_sb[t + 1][:], in1=gate[t + 1][:], op=ALU.mult)
+                nc.gpsimd.tensor_tensor(out=st[t + 1], in0=h_sb[t + 1], in1=gate[t + 1][:], op=ALU.mult)
             for cols in ([slice(0, S)] if t < last else halves):
                 nc.vector.tensor_tensor(out=res[t][:, cols], in0=st[t][:, cols], in1=far[t][:, cols], op=ALU.max)
                 nc.sync.dma_start(out_rows[:, t, cols], res[t][:, cols])

@@ -71,12 +71,15 @@ def tile_picked_layquadtwicp_none_p_kernel(tc, x_words, x_scales, w1, gn, w2, of
         nc.vector.tensor_copy(out=x_codes[:], in_=x_table[:].indirect(offs_t[:]))
         nc.vector.tensor_copy(out=x_scale[:], in_=s_table[:].indirect(offs_t[:]))
 
-        def deal(copy, raw, pair, name):
+        def deal(copies, raw, pair, name):
             grouped = sb(name, [P, 2, P, PACK], BF16)
-            copy(
-                out=grouped[:].rearrange("p e m j -> p m j e"),
-                in_=raw[:].rearrange("p j (m u e) -> p u m j e", u=2, e=2)[:, pair],
-            )
+            share = P // len(copies)
+            for i, copy in enumerate(copies):
+                m_cols = slice(i * share, (i + 1) * share)
+                copy(
+                    out=grouped[:].rearrange("p e m j -> p m j e")[:, m_cols],
+                    in_=raw[:].rearrange("p j (m u e) -> p u m j e", u=2, e=2)[:, pair, m_cols],
+                )
             return grouped
 
         def quantize(flat, width, name):
@@ -97,9 +100,13 @@ def tile_picked_layquadtwicp_none_p_kernel(tc, x_words, x_scales, w1, gn, w2, of
             )
 
         every = slice(0, P)
-        w1_lo = deal(nc.vector.tensor_copy, w1_raw, 0, "w1_lo")
-        w1_hi = deal(nc.scalar.copy, w1_raw, 1, "w1_hi")
-        w1_q = [quantize(w1_lo[:, e].rearrange("p m j -> p (m j)"), P, "w1_q%d" % e) for e in range(2)]
+        w1_lo = deal([nc.vector.tensor_copy, nc.vector.tensor_copy], w1_raw, 0, "w1_lo")
+        w1_hi = deal([nc.scalar.copy], w1_raw, 1, "w1_hi")
+        first_codes = sb("first_codes", [P, P], U32)
+        first_scale = sb("first_scale", [P, P], U8)
+        for m_cols in (slice(0, P // 2), slice(P // 2, P)):
+            nc.vector.quantize_mx(out=first_codes[:, m_cols].bitcast(FP8X4), scales=first_scale[:, m_cols], in_=w1_lo[:, 0, m_cols].rearrange("p m j -> p (m j)"))
+        w1_q = [(first_codes, first_scale), quantize(w1_lo[:, 1].rearrange("p m j -> p (m j)"), P, "w1_q1")]
         w1_q_hi = quantize(w1_hi[:].rearrange("p e m j -> p (e m j)"), 2 * P, "w1_q_hi")
         w1_ops = [(w1_q[0], every), (w1_q[1], every), (w1_q_hi, slice(0, P)), (w1_q_hi, slice(P, 2 * P))]
         x_q = (x_codes, x_scale)
@@ -118,7 +125,8 @@ def tile_picked_layquadtwicp_none_p_kernel(tc, x_words, x_scales, w1, gn, w2, of
             nc.scalar.copy(out=y_win[t][:, 0:S], in_=acc[:])
             nc.scalar.copy(out=y_own[t], in_=acc[:])
 
-        d1 = [sb("d1_%d" % t, [P, S], F32) for t in range(PACK)]
+        h_win = [None] + [sb("h_win%d" % t, [P, 2 * S], F32) for t in range(1, PACK)]
+        d1 = [sb("d1_0", [P, S], F32)[:]] + [h_win[t][:, S : 2 * S] for t in range(1, PACK)]
         d1g = sb("d1g", [P, PACK, S], F32)
         d2 = sb("d2", [P, PACK, S], F32)
         last = PACK - 1
@@ -130,54 +138,66 @@ def tile_picked_layquadtwicp_none_p_kernel(tc, x_words, x_scales, w1, gn, w2, of
         def difference(dst, t, lists, cols):
             nc.vector.tensor_tensor(out=dst[:, cols], in0=y_win[t][:].indirect(entries(lists, cols)), in1=y_own[t][:, cols], op=ALU.subtract)
 
+        z_codes = sb("z_codes", [P, S], U32)
+        z_scale = sb("z_scale", [P, S], U8)
+        z_q = (z_codes, z_scale)
+        pieces = [slice(0, HALF), slice(HALF, HALF + P), slice(HALF + P, S)]
+        z = [sb("z%d" % c, [P, cols.stop - cols.start, PACK], BF16) for c, cols in enumerate(pieces)]
+
         def hidden(c):
-            z = sb("z%d" % c, [P, HALF, PACK], BF16)
             nc.vector.tensor_tensor(
-                out=z[:].rearrange("p (a i) t -> p a t i", i=2),
-                in0=d1g[:, :, halves[c]].rearrange("p t (a i) -> p a t i", i=2),
-                in1=d2[:, :, halves[c]].rearrange("p t (a i) -> p a t i", i=2),
+                out=z[c][:].rearrange("p (a i) t -> p a t i", i=2),
+                in0=d1g[:, :, pieces[c]].rearrange("p t (a i) -> p a t i", i=2),
+                in1=d2[:, :, pieces[c]].rearrange("p t (a i) -> p a t i", i=2),
                 op=ALU.mult,
             )
-            return z[:].rearrange("p j t -> p (j t)")
+
+        def quantize_hidden(c):
+            nc.vector.quantize_mx(out=z_codes[:, pieces[c]].bitcast(FP8X4), scales=z_scale[:, pieces[c]], in_=z[c][:].rearrange("p j t -> p (j t)"))
 
         for t in range(PACK):
             for cols in (halves if t == 0 else [whole]):
                 difference(d1[t], t, n1_t, cols)
-            nc.scalar.activation(out=d1g[:, t, :], in_=d1[t][:], func=ACT.Copy, scale=gain[:, t : t + 1])
+            nc.scalar.activation(out=d1g[:, t, :], in_=d1[t], func=ACT.Copy, scale=gain[:, t : t + 1])
             if t < last:
                 for cols in (halves if t == 0 else [whole]):
                     difference(d2[:, t, :], t, n2_t, cols)
-        w2_lo = deal(nc.scalar.copy, w2_raw, 0, "w2_lo")
-        w2_hi = deal(nc.scalar.copy, w2_raw, 1, "w2_hi")
+        w2_lo = deal([nc.scalar.copy], w2_raw, 0, "w2_lo")
+        w2_hi = deal([nc.scalar.copy], w2_raw, 1, "w2_hi")
         difference(d2[:, last, :], last, n2_t, halves[0])
         w2_q_lo = quantize(w2_lo[:].rearrange("p e m j -> p (e m j)"), 2 * P, "w2_q_lo")
-        z0 = hidden(0)
+        hidden(0)
         difference(d2[:, last, :], last, n2_t, halves[1])
-        z_q = [quantize(z0, HALF, "z_q0")]
-        z1 = hidden(1)
-        z_q.append(quantize(z1, HALF, "z_q1"))
+        quantize_hidden(0)
+        hidden(1)
+        hidden(2)
+        quantize_hidden(1)
+        quantize_hidden(2)
         w2_q_hi = quantize(w2_hi[:].rearrange("p e m j -> p (e m j)"), 2 * P, "w2_q_hi")
         w2_ops = [(w2_q_lo, slice(0, P)), (w2_q_lo, slice(P, 2 * P)), (w2_q_hi, slice(0, P)), (w2_q_hi, slice(P, 2 * P))]
 
         st_win = [sb("st_win%d" % t, [P, 2 * S], F32) for t in range(PACK)]
-        h_sb = [st_win[0][:, S : 2 * S]] + [sb("h%d" % t, [P, S], F32)[:] for t in range(1, PACK)]
+        h_sb = [st_win[0][:, S : 2 * S]] + [h_win[t][:, 0:S] for t in range(1, PACK)]
         gate = [sb("gate%d" % t, [P, S], F32) for t in range(PACK)]
-        h_acc = [bank((5 + t) % 8, "h_acc%d" % t) for t in range(PACK)]
-        for c in range(2):
-            for t in range(2):
-                product(h_acc[t][:, halves[c]], w2_ops[t][0], w2_ops[t][1], z_q[c], slice(0, HALF))
-                if t == 0:
-                    nc.scalar.activation(out=gate[0][:, halves[c]], in_=h_acc[0][:, halves[c]], func=ACT.Sigmoid)
-                nc.scalar.copy(out=h_sb[t][:, halves[c]], in_=h_acc[t][:, halves[c]])
-        for t in range(2, PACK):
-            for c in range(2):
-                product(h_acc[t][:, halves[c]], w2_ops[t][0], w2_ops[t][1], z_q[c], slice(0, HALF))
+
+        def second_layer(t, cols, b, copy=nc.scalar.copy):
+            width = cols.stop - cols.start
+            acc = bank(b, "h%d_%d" % (t, cols.start))[:, 0:width]
+            product(acc, w2_ops[t][0], w2_ops[t][1], z_q, cols)
+            if t == 0:
+                nc.scalar.activation(out=gate[0][:, cols], in_=acc, func=ACT.Sigmoid)
+            copy(out=h_sb[t][:, cols], in_=acc)
+
+        second_layer(0, pieces[0], 5)
+        second_layer(1, halves[0], 0)
+        second_layer(0, pieces[1], 6, nc.vector.tensor_copy)
+        second_layer(0, pieces[2], 7)
+        second_layer(1, halves[1], 1)
 
         def gates(t):
             if t >= 2:
-                nc.scalar.copy(out=h_sb[t], in_=h_acc[t][:])
-            for c in range(2):
-                nc.scalar.activation(out=gate[t][:, halves[c]], in_=h_sb[t].indirect(n3_t[:, list_halves[c]]), func=ACT.Sigmoid)
+                second_layer(t, whole, t)
+            nc.scalar.activation(out=gate[t][:], in_=h_win[t][:].indirect(n3_t[:]), func=ACT.Sigmoid)
 
         st = [st_win[t][:, 0:S] for t in range(PACK)]
         far = [st_win[t + 1][:, S : 2 * S] for t in range(PACK - 1)] + [sb("far_last", [P, S], F32)[:]]
@@ -191,7 +211,7 @@ def tile_picked_layquadtwicp_none_p_kernel(tc, x_words, x_scales, w1, gn, w2, of
                 nc.vector.tensor_copy(out=far[t][:, cols], in_=st_win[t][:].indirect(entries(n3_t, cols)))
             if t < last:
                 gates(t + 1)
-                nc.gpsimd.tensor_tensor(out=st[t + 1], in0=h_sb[t + 1], in1=gate[t + 1][:], op=ALU.mult)
+                nc.vector.tensor_tensor(out=st[t + 1], in0=h_sb[t + 1], in1=gate[t + 1][:], op=ALU.mult)
             for cols in ([slice(0, S)] if t < last else halves):
                 nc.vector.tensor_tensor(out=res[t][:, cols], in0=st[t][:, cols], in1=far[t][:, cols], op=ALU.max)
                 nc.sync.dma_start(out_rows[:, t, cols], res[t][:, cols])

@@ -19,12 +19,15 @@ P = 128
 PACK = 4
 HALF = S // 2
 LIST_ROWS = 16
+QUADRANT = 32
 
 
 def tile_picked_layquadtwicp_none_p_kernel(tc, x_words, x_scales, w1, gn, w2, offs, n1, n2, n3, out):
     nc = tc.nc
+    whole = slice(0, S)
     halves = [slice(0, HALF), slice(HALF, S)]
-    list_halves = [slice(0, HALF // LIST_ROWS), slice(HALF // LIST_ROWS, S // LIST_ROWS)]
+    right = slice(S, 2 * S)
+    last = PACK - 1
 
     with ExitStack() as ctx:
         keep = ctx.enter_context(tc.tile_pool(name="keep", bufs=1))
@@ -36,6 +39,9 @@ def tile_picked_layquadtwicp_none_p_kernel(tc, x_words, x_scales, w1, gn, w2, of
         def bank(b, name):
             return psum.tile([P, S], F32, name=name, tag="bank%d" % b)
 
+        def entries(lists, cols):
+            return lists[:, cols.start // LIST_ROWS : cols.stop // LIST_ROWS]
+
         offs_t = sb("offs_t", [P, S // LIST_ROWS], U16)
         n1_t = sb("n1_t", [P, S // LIST_ROWS], U16)
         n2_t = sb("n2_t", [P, S // LIST_ROWS], U16)
@@ -44,174 +50,177 @@ def tile_picked_layquadtwicp_none_p_kernel(tc, x_words, x_scales, w1, gn, w2, of
         s_table = sb("s_table", [P, T], U8)
         w1_raw = sb("w1_raw", [P, PACK, H], F32)
         w2_raw = sb("w2_raw", [P, PACK, N], F32)
-        gain_raw = sb("gain_raw", [P, PACK], F32)
+        gn_raw = sb("gn_raw", [P, PACK], F32)
         gain = sb("gain", [P, PACK], F32)
-        warm_in = sb("warm_in", [P, 1], F32)
-        warm_out = sb("warm_out", [P, 1], F32)
 
         nc.vector.memset(s_table[:].bitcast(I32), 0)
-        nc.vector.memset(warm_in[:], 0.0)
-        nc.scalar.activation(out=warm_out[:], in_=warm_in[:], func=ACT.Sigmoid)
 
         nc.sync.dma_start(x_table[:].bitcast(I32), x_words[0].rearrange("p n t -> p (n t)").bitcast(I32))
         nc.sync.dma_start(offs_t[:], offs)
-        for q in range(4):
-            nc.sync.dma_start(s_table[32 * q : 32 * q + 4, :].bitcast(I32), x_scales[0, 4 * q : 4 * q + 4, :].bitcast(I32))
+        for q in range(P // QUADRANT):
+            nc.sync.dma_start(s_table[QUADRANT * q : QUADRANT * q + PACK, :].bitcast(I32), x_scales[0, PACK * q : PACK * q + PACK, :].bitcast(I32))
         nc.sync.dma_start(w1_raw[:], w1.rearrange("(p j) c -> p j c", j=PACK))
         nc.sync.dma_start(n1_t[:], n1)
         nc.sync.dma_start(n2_t[:], n2)
-        nc.sync.dma_start(gain_raw[:], gn.rearrange("(p t) o -> p (t o)", t=PACK))
+        nc.sync.dma_start(gn_raw[:], gn.rearrange("(p t) o -> p (t o)", t=PACK))
         nc.sync.dma_start(w2_raw[:], w2.rearrange("(p j) c -> p j c", j=PACK))
         nc.sync.dma_start(n3_t[:], n3)
 
-        nc.gpsimd.tensor_scalar(out=gain[:], in0=gain_raw[:], scalar1=0.75, scalar2=0.0, op0=ALU.mult, op1=ALU.add)
+        nc.gpsimd.tensor_scalar(out=gain[:], in0=gn_raw[:], scalar1=0.75, scalar2=0.0, op0=ALU.mult, op1=ALU.add)
 
         x_codes = sb("x_codes", [P, S], U32)
         x_scale = sb("x_scale", [P, S], U8)
         nc.vector.tensor_copy(out=x_codes[:], in_=x_table[:].indirect(offs_t[:]))
         nc.vector.tensor_copy(out=x_scale[:], in_=s_table[:].indirect(offs_t[:]))
+        x_q = (x_codes, x_scale)
 
-        def deal(copies, raw, pair, name):
-            grouped = sb(name, [P, 2, P, PACK], BF16)
-            share = P // len(copies)
-            for i, copy in enumerate(copies):
-                m_cols = slice(i * share, (i + 1) * share)
+        def deal(copy, raw, pair, name, parts):
+            dealt = sb(name, [P, 2, P, PACK], BF16)
+            for i in range(parts):
+                m_cols = slice(i * P // parts, (i + 1) * P // parts)
                 copy(
-                    out=grouped[:].rearrange("p e m j -> p m j e")[:, m_cols],
+                    out=dealt[:].rearrange("p e m j -> p m j e")[:, m_cols],
                     in_=raw[:].rearrange("p j (m u e) -> p u m j e", u=2, e=2)[:, pair, m_cols],
                 )
-            return grouped
+            return dealt
 
-        def quantize(flat, width, name):
-            codes = sb(name + "_codes", [P, width], U32)
-            scale = sb(name + "_scale", [P, width], U8)
-            nc.vector.quantize_mx(out=codes[:].bitcast(FP8X4), scales=scale[:], in_=flat)
-            return codes, scale
+        def packed(name, width):
+            return sb(name + "_codes", [P, width], U32), sb(name + "_scale", [P, width], U8)
 
-        def product(acc, stationary, m_cols, moving, n_cols):
+        def quantize(operand, cols, values):
+            nc.vector.quantize_mx(out=operand[0][:, cols].bitcast(FP8X4), scales=operand[1][:, cols], in_=values)
+
+        def quantize_pair(dealt, name):
+            operand = packed(name, 2 * P)
+            quantize(operand, slice(0, 2 * P), dealt[:].rearrange("p e m j -> p (e m j)"))
+            return [(operand, slice(0, P)), (operand, slice(P, 2 * P))]
+
+        def product(acc, stationary, moving, n_cols):
+            (codes, scale), m_cols = stationary
             nc.tensor.matmul_mx(
                 out=acc,
-                lhsT=stationary[0][:, m_cols].bitcast(FP8X4),
-                lhsT_scale=stationary[1][:, m_cols],
+                lhsT=codes[:, m_cols].bitcast(FP8X4),
+                lhsT_scale=scale[:, m_cols],
                 rhs=moving[0][:, n_cols].bitcast(FP8X4),
                 rhs_scale=moving[1][:, n_cols],
                 start=True,
                 stop=True,
             )
 
-        every = slice(0, P)
-        w1_lo = deal([nc.vector.tensor_copy, nc.vector.tensor_copy], w1_raw, 0, "w1_lo")
-        w1_hi = deal([nc.scalar.copy], w1_raw, 1, "w1_hi")
-        first_codes = sb("first_codes", [P, P], U32)
-        first_scale = sb("first_scale", [P, P], U8)
+        w1_lo = deal(nc.vector.tensor_copy, w1_raw, 0, "w1_lo", 2)
+        w1_hi = deal(nc.scalar.copy, w1_raw, 1, "w1_hi", 1)
+        w1_q0 = packed("w1_q0", P)
         for m_cols in (slice(0, P // 2), slice(P // 2, P)):
-            nc.vector.quantize_mx(out=first_codes[:, m_cols].bitcast(FP8X4), scales=first_scale[:, m_cols], in_=w1_lo[:, 0, m_cols].rearrange("p m j -> p (m j)"))
-        w1_q = [(first_codes, first_scale), quantize(w1_lo[:, 1].rearrange("p m j -> p (m j)"), P, "w1_q1")]
-        w1_q_hi = quantize(w1_hi[:].rearrange("p e m j -> p (e m j)"), 2 * P, "w1_q_hi")
-        w1_ops = [(w1_q[0], every), (w1_q[1], every), (w1_q_hi, slice(0, P)), (w1_q_hi, slice(P, 2 * P))]
-        x_q = (x_codes, x_scale)
+            quantize(w1_q0, m_cols, w1_lo[:, 0, m_cols].rearrange("p m j -> p (m j)"))
+        w1_q1 = packed("w1_q1", P)
+        quantize(w1_q1, slice(0, P), w1_lo[:, 1].rearrange("p m j -> p (m j)"))
+        w1_q = [(w1_q0, slice(0, P)), (w1_q1, slice(0, P))] + quantize_pair(w1_hi, "w1_q23")
 
         y_win = [sb("y_win%d" % t, [P, S if t == 0 else 2 * S], F32) for t in range(PACK)]
         y_last = sb("y_last", [P, S], F32)
-        y_own = [y_win[t + 1][:, S : 2 * S] for t in range(PACK - 1)] + [y_last[:]]
+        y_own = [y_win[t + 1][:, right] for t in range(last)] + [y_last[:]]
         for c, copy in enumerate((nc.scalar.copy, nc.vector.tensor_copy)):
-            acc = bank(c, "y0_%d" % c)
-            product(acc[:, 0:HALF], w1_ops[0][0], w1_ops[0][1], x_q, halves[c])
-            copy(out=y_win[0][:, halves[c]], in_=acc[:, 0:HALF])
-            nc.scalar.copy(out=y_own[0][:, halves[c]], in_=acc[:, 0:HALF])
+            acc = bank(c, "y0_%d" % c)[:, 0:HALF]
+            product(acc, w1_q[0], x_q, halves[c])
+            copy(out=y_win[0][:, halves[c]], in_=acc)
+            nc.scalar.copy(out=y_own[0][:, halves[c]], in_=acc)
         for t in range(1, PACK):
-            acc = bank(1 + t, "y%d" % t)
-            product(acc[:], w1_ops[t][0], w1_ops[t][1], x_q, slice(0, S))
-            nc.scalar.copy(out=y_win[t][:, 0:S], in_=acc[:])
-            nc.scalar.copy(out=y_own[t], in_=acc[:])
+            acc = bank(1 + t, "y%d" % t)[:]
+            product(acc, w1_q[t], x_q, whole)
+            nc.scalar.copy(out=y_win[t][:, whole], in_=acc)
+            nc.scalar.copy(out=y_own[t], in_=acc)
 
-        h_win = [None] + [sb("h_win%d" % t, [P, 2 * S], F32) for t in range(1, PACK)]
-        d1 = [sb("d1_0", [P, S], F32)[:]] + [h_win[t][:, S : 2 * S] for t in range(1, PACK)]
-        d1g = sb("d1g", [P, PACK, S], F32)
+        st_win = [sb("st_win%d" % t, [P, 2 * S if t < last else S], F32) for t in range(PACK)]
+        h_win = {t: sb("h_win%d" % t, [P, 2 * S], F32) for t in range(2, PACK)}
+        d1 = [st_win[1][:, right], st_win[2][:, right], h_win[2][:, right], h_win[3][:, right]]
+        d1_gained = sb("d1_gained", [P, PACK, S], F32)
         d2 = sb("d2", [P, PACK, S], F32)
-        last = PACK - 1
-        whole = slice(0, S)
-
-        def entries(lists, cols):
-            return lists[:, cols.start // LIST_ROWS : cols.stop // LIST_ROWS]
 
         def difference(dst, t, lists, cols):
             nc.vector.tensor_tensor(out=dst[:, cols], in0=y_win[t][:].indirect(entries(lists, cols)), in1=y_own[t][:, cols], op=ALU.subtract)
 
-        z_codes = sb("z_codes", [P, S], U32)
-        z_scale = sb("z_scale", [P, S], U8)
-        z_q = (z_codes, z_scale)
-        pieces = [slice(0, HALF), slice(HALF, HALF + P), slice(HALF + P, S)]
+        z_q = packed("z", S)
+        pieces = [halves[0], slice(HALF, HALF + P), slice(HALF + P, S)]
         z = [sb("z%d" % c, [P, cols.stop - cols.start, PACK], BF16) for c, cols in enumerate(pieces)]
 
         def hidden(c):
             nc.vector.tensor_tensor(
                 out=z[c][:].rearrange("p (a i) t -> p a t i", i=2),
-                in0=d1g[:, :, pieces[c]].rearrange("p t (a i) -> p a t i", i=2),
+                in0=d1_gained[:, :, pieces[c]].rearrange("p t (a i) -> p a t i", i=2),
                 in1=d2[:, :, pieces[c]].rearrange("p t (a i) -> p a t i", i=2),
                 op=ALU.mult,
             )
 
         def quantize_hidden(c):
-            nc.vector.quantize_mx(out=z_codes[:, pieces[c]].bitcast(FP8X4), scales=z_scale[:, pieces[c]], in_=z[c][:].rearrange("p j t -> p (j t)"))
+            quantize(z_q, pieces[c], z[c][:].rearrange("p j t -> p (j t)"))
 
         for t in range(PACK):
             for cols in (halves if t == 0 else [whole]):
                 difference(d1[t], t, n1_t, cols)
-            nc.scalar.activation(out=d1g[:, t, :], in_=d1[t], func=ACT.Copy, scale=gain[:, t : t + 1])
-            if t < last:
-                for cols in (halves if t == 0 else [whole]):
-                    difference(d2[:, t, :], t, n2_t, cols)
-        w2_lo = deal([nc.scalar.copy], w2_raw, 0, "w2_lo")
-        w2_hi = deal([nc.scalar.copy], w2_raw, 1, "w2_hi")
-        difference(d2[:, last, :], last, n2_t, halves[0])
-        w2_q_lo = quantize(w2_lo[:].rearrange("p e m j -> p (e m j)"), 2 * P, "w2_q_lo")
+            nc.scalar.activation(out=d1_gained[:, t, :], in_=d1[t], func=ACT.Copy, scale=gain[:, t : t + 1])
+            difference(d2[:, t, :], t, n2_t, halves[0])
+        w2_lo = deal(nc.scalar.copy, w2_raw, 0, "w2_lo", 1)
+        w2_hi = deal(nc.scalar.copy, w2_raw, 1, "w2_hi", 1)
+        difference(d2[:, 0, :], 0, n2_t, halves[1])
         hidden(0)
-        difference(d2[:, last, :], last, n2_t, halves[1])
+        w2_q = quantize_pair(w2_lo, "w2_q01")
         quantize_hidden(0)
+        for t in range(1, PACK):
+            difference(d2[:, t, :], t, n2_t, halves[1])
+        w2_q = w2_q + quantize_pair(w2_hi, "w2_q23")
         hidden(1)
         hidden(2)
         quantize_hidden(1)
         quantize_hidden(2)
-        w2_q_hi = quantize(w2_hi[:].rearrange("p e m j -> p (e m j)"), 2 * P, "w2_q_hi")
-        w2_ops = [(w2_q_lo, slice(0, P)), (w2_q_lo, slice(P, 2 * P)), (w2_q_hi, slice(0, P)), (w2_q_hi, slice(P, 2 * P))]
 
-        st_win = [sb("st_win%d" % t, [P, 2 * S], F32) for t in range(PACK)]
-        h_sb = [st_win[0][:, S : 2 * S]] + [h_win[t][:, 0:S] for t in range(1, PACK)]
+        shared = sb("shared", [P, S + HALF], F32)
+        h_sb = [st_win[0][:, right], shared[:, HALF : HALF + S], h_win[2][:, whole], h_win[3][:, whole]]
         gate = [sb("gate%d" % t, [P, S], F32) for t in range(PACK)]
 
-        def second_layer(t, cols, b, copy=nc.scalar.copy):
-            width = cols.stop - cols.start
-            acc = bank(b, "h%d_%d" % (t, cols.start))[:, 0:width]
-            product(acc, w2_ops[t][0], w2_ops[t][1], z_q, cols)
-            if t == 0:
-                nc.scalar.activation(out=gate[0][:, cols], in_=acc, func=ACT.Sigmoid)
+        def second_layer(t, cols, b, copy):
+            acc = bank(b, "h%d_%d" % (t, cols.start))[:, 0 : cols.stop - cols.start]
+            product(acc, w2_q[t], z_q, cols)
+            if t not in h_win:
+                nc.scalar.activation(out=gate[t][:, cols], in_=acc, func=ACT.Sigmoid)
             copy(out=h_sb[t][:, cols], in_=acc)
+            return acc
 
-        second_layer(0, pieces[0], 5)
-        second_layer(1, halves[0], 0)
+        second_layer(0, pieces[0], 5, nc.scalar.copy)
+        second_layer(1, halves[0], 0, nc.scalar.copy)
         second_layer(0, pieces[1], 6, nc.vector.tensor_copy)
-        second_layer(0, pieces[2], 7)
-        second_layer(1, halves[1], 1)
-
-        def gates(t):
-            if t >= 2:
-                second_layer(t, whole, t)
+        second_layer(0, pieces[2], 7, nc.scalar.copy)
+        second_layer(1, halves[1], 1, nc.scalar.copy)
+        h_acc = {}
+        for t in h_win:
+            h_acc[t] = second_layer(t, whole, t, nc.scalar.copy)
             nc.scalar.activation(out=gate[t][:], in_=h_win[t][:].indirect(n3_t[:]), func=ACT.Sigmoid)
 
-        st = [st_win[t][:, 0:S] for t in range(PACK)]
-        far = [st_win[t + 1][:, S : 2 * S] for t in range(PACK - 1)] + [sb("far_last", [P, S], F32)[:]]
+        st = [st_win[t][:, whole] for t in range(PACK)]
+        far = [shared[:, whole], st[last], sb("far2", [P, S], F32)[:], sb("far3", [P, S], F32)[:]]
         res = [sb("res%d" % t, [P, S], F32) for t in range(PACK)]
         out_rows = out.rearrange("(p t) c -> p t c", t=PACK)
 
-        for c in range(2):
-            nc.vector.tensor_tensor(out=st[0][:, halves[c]], in0=gate[0][:].indirect(n3_t[:, list_halves[c]]), in1=h_sb[0][:, halves[c]], op=ALU.mult)
-        for t in range(PACK):
-            for cols in ([whole] if t < last else halves):
-                nc.vector.tensor_copy(out=far[t][:, cols], in_=st_win[t][:].indirect(entries(n3_t, cols)))
-            if t < last:
-                gates(t + 1)
-                nc.vector.tensor_tensor(out=st[t + 1], in0=h_sb[t + 1], in1=gate[t + 1][:], op=ALU.mult)
-            for cols in ([slice(0, S)] if t < last else halves):
-                nc.vector.tensor_tensor(out=res[t][:, cols], in0=st[t][:, cols], in1=far[t][:, cols], op=ALU.max)
-                nc.sync.dma_start(out_rows[:, t, cols], res[t][:, cols])
+        def fetch(t, cols):
+            nc.vector.tensor_copy(out=far[t][:, cols], in_=st_win[t][:].indirect(entries(n3_t, cols)))
+
+        def larger(t, cols):
+            nc.vector.tensor_tensor(out=res[t][:, cols], in0=st[t][:, cols], in1=far[t][:, cols], op=ALU.max)
+            nc.sync.dma_start(out_rows[:, t, cols], res[t][:, cols])
+
+        for t in range(2):
+            for cols in halves:
+                nc.vector.tensor_tensor(out=st[t][:, cols], in0=gate[t][:].indirect(entries(n3_t, cols)), in1=h_sb[t][:, cols], op=ALU.mult)
+        nc.gpsimd.tensor_tensor(out=st[2], in0=h_sb[2], in1=gate[2][:], op=ALU.mult)
+        fetch(0, whole)
+        fetch(1, whole)
+        larger(0, whole)
+        larger(1, whole)
+        head, tail = slice(0, S - S // 4), slice(S - S // 4, S)
+        nc.gpsimd.tensor_tensor(out=st[last][:, head], in0=h_sb[last][:, head], in1=gate[last][:, head], op=ALU.mult)
+        fetch(2, whole)
+        nc.vector.tensor_tensor(out=st[last][:, tail], in0=h_acc[last][:, tail], in1=gate[last][:, tail], op=ALU.mult)
+        larger(2, whole)
+        for cols in halves:
+            fetch(last, cols)
+        for cols in halves:
+            larger(last, cols)

from contextlib import ExitStack

import concourse.mybir as mybir

K, T, S, N, H = 512, 2048, 512, 512, 512
FLOPS = 2 * K * H * S + 2 * H * N * S

F32 = mybir.dt.float32
BF16 = mybir.dt.bfloat16
I32 = mybir.dt.int32
U32 = mybir.dt.uint32
U16 = mybir.dt.uint16
U8 = mybir.dt.uint8
FP8X4 = mybir.dt.float8_e4m3fn_x4
ALU = mybir.AluOpType
ACT = mybir.ActivationFunctionType

P = 128
PACK = 4
HALF = S // 2
LIST_ROWS = 16
QUADRANT = 32


def tile_picked_layquadtwicp_none_p_kernel(tc, x_words, x_scales, w1, gn, w2, offs, n1, n2, n3, out):
    nc = tc.nc
    whole = slice(0, S)
    halves = [slice(0, HALF), slice(HALF, S)]
    right = slice(S, 2 * S)
    last = PACK - 1

    with ExitStack() as ctx:
        keep = ctx.enter_context(tc.tile_pool(name="keep", bufs=1))
        psum = ctx.enter_context(tc.psum_pool(name="psum", bufs=1))

        def sb(name, shape, dtype):
            return keep.tile(shape, dtype, name=name, align_bytes=64)

        def bank(b, name):
            return psum.tile([P, S], F32, name=name, tag="bank%d" % b)

        def entries(lists, cols):
            return lists[:, cols.start // LIST_ROWS : cols.stop // LIST_ROWS]

        offs_t = sb("offs_t", [P, S // LIST_ROWS], U16)
        n1_t = sb("n1_t", [P, S // LIST_ROWS], U16)
        n2_t = sb("n2_t", [P, S // LIST_ROWS], U16)
        n3_t = sb("n3_t", [P, S // LIST_ROWS], U16)
        x_table = sb("x_table", [P, T], U32)
        s_table = sb("s_table", [P, T], U8)
        w1_raw = sb("w1_raw", [P, PACK, H], F32)
        w2_raw = sb("w2_raw", [P, PACK, N], F32)
        gn_raw = sb("gn_raw", [P, PACK], F32)
        gain = sb("gain", [P, PACK], F32)

        nc.vector.memset(s_table[:].bitcast(I32), 0)

        nc.sync.dma_start(x_table[:].bitcast(I32), x_words[0].rearrange("p n t -> p (n t)").bitcast(I32))
        nc.sync.dma_start(offs_t[:], offs)
        for q in range(P // QUADRANT):
            nc.sync.dma_start(s_table[QUADRANT * q : QUADRANT * q + PACK, :].bitcast(I32), x_scales[0, PACK * q : PACK * q + PACK, :].bitcast(I32))
        nc.sync.dma_start(w1_raw[:], w1.rearrange("(p j) c -> p j c", j=PACK))
        nc.sync.dma_start(n1_t[:], n1)
        nc.sync.dma_start(n2_t[:], n2)
        nc.sync.dma_start(gn_raw[:], gn.rearrange("(p t) o -> p (t o)", t=PACK))
        nc.sync.dma_start(w2_raw[:], w2.rearrange("(p j) c -> p j c", j=PACK))
        nc.sync.dma_start(n3_t[:], n3)

        nc.gpsimd.tensor_scalar(out=gain[:], in0=gn_raw[:], scalar1=0.75, scalar2=0.0, op0=ALU.mult, op1=ALU.add)

        x_codes = sb("x_codes", [P, S], U32)
        x_scale = sb("x_scale", [P, S], U8)
        nc.vector.tensor_copy(out=x_codes[:], in_=x_table[:].indirect(offs_t[:]))
        nc.vector.tensor_copy(out=x_scale[:], in_=s_table[:].indirect(offs_t[:]))
        x_q = (x_codes, x_scale)

        def deal(copy, raw, pair, name, parts):
            dealt = sb(name, [P, 2, P, PACK], BF16)
            for i in range(parts):
                m_cols = slice(i * P // parts, (i + 1) * P // parts)
                copy(
                    out=dealt[:].rearrange("p e m j -> p m j e")[:, m_cols],
                    in_=raw[:].rearrange("p j (m u e) -> p u m j e", u=2, e=2)[:, pair, m_cols],
                )
            return dealt

        def packed(name, width):
            return sb(name + "_codes", [P, width], U32), sb(name + "_scale", [P, width], U8)

        def quantize(operand, cols, values):
            nc.vector.quantize_mx(out=operand[0][:, cols].bitcast(FP8X4), scales=operand[1][:, cols], in_=values)

        def quantize_pair(dealt, name):
            operand = packed(name, 2 * P)
            quantize(operand, slice(0, 2 * P), dealt[:].rearrange("p e m j -> p (e m j)"))
            return [(operand, slice(0, P)), (operand, slice(P, 2 * P))]

        def product(acc, stationary, moving, n_cols):
            (codes, scale), m_cols = stationary
            nc.tensor.matmul_mx(
                out=acc,
                lhsT=codes[:, m_cols].bitcast(FP8X4),
                lhsT_scale=scale[:, m_cols],
                rhs=moving[0][:, n_cols].bitcast(FP8X4),
                rhs_scale=moving[1][:, n_cols],
                start=True,
                stop=True,
            )

        w1_lo = deal(nc.vector.tensor_copy, w1_raw, 0, "w1_lo", 2)
        w1_hi = deal(nc.scalar.copy, w1_raw, 1, "w1_hi", 1)
        w1_q0 = packed("w1_q0", P)
        for m_cols in (slice(0, P // 2), slice(P // 2, P)):
            quantize(w1_q0, m_cols, w1_lo[:, 0, m_cols].rearrange("p m j -> p (m j)"))
        w1_q1 = packed("w1_q1", P)
        quantize(w1_q1, slice(0, P), w1_lo[:, 1].rearrange("p m j -> p (m j)"))
        w1_q = [(w1_q0, slice(0, P)), (w1_q1, slice(0, P))] + quantize_pair(w1_hi, "w1_q23")

        y_win = [sb("y_win%d" % t, [P, S if t == 0 else 2 * S], F32) for t in range(PACK)]
        y_last = sb("y_last", [P, S], F32)
        y_own = [y_win[t + 1][:, right] for t in range(last)] + [y_last[:]]
        for c, copy in enumerate((nc.scalar.copy, nc.vector.tensor_copy)):
            acc = bank(c, "y0_%d" % c)[:, 0:HALF]
            product(acc, w1_q[0], x_q, halves[c])
            copy(out=y_win[0][:, halves[c]], in_=acc)
            nc.scalar.copy(out=y_own[0][:, halves[c]], in_=acc)
        for t in range(1, PACK):
            acc = bank(1 + t, "y%d" % t)[:]
            product(acc, w1_q[t], x_q, whole)
            nc.scalar.copy(out=y_win[t][:, whole], in_=acc)
            nc.scalar.copy(out=y_own[t], in_=acc)

        st_win = [sb("st_win%d" % t, [P, 2 * S if t < last else S], F32) for t in range(PACK)]
        h_win = {t: sb("h_win%d" % t, [P, 2 * S], F32) for t in range(2, PACK)}
        d1 = [st_win[1][:, right], st_win[2][:, right], h_win[2][:, right], h_win[3][:, right]]
        d1_gained = sb("d1_gained", [P, PACK, S], F32)
        d2 = sb("d2", [P, PACK, S], F32)

        def difference(dst, t, lists, cols):
            nc.vector.tensor_tensor(out=dst[:, cols], in0=y_win[t][:].indirect(entries(lists, cols)), in1=y_own[t][:, cols], op=ALU.subtract)

        z_q = packed("z", S)
        pieces = [halves[0], slice(HALF, HALF + P), slice(HALF + P, S)]
        z = [sb("z%d" % c, [P, cols.stop - cols.start, PACK], BF16) for c, cols in enumerate(pieces)]

        def hidden(c):
            nc.vector.tensor_tensor(
                out=z[c][:].rearrange("p (a i) t -> p a t i", i=2),
                in0=d1_gained[:, :, pieces[c]].rearrange("p t (a i) -> p a t i", i=2),
                in1=d2[:, :, pieces[c]].rearrange("p t (a i) -> p a t i", i=2),
                op=ALU.mult,
            )

        def quantize_hidden(c):
            quantize(z_q, pieces[c], z[c][:].rearrange("p j t -> p (j t)"))

        for t in range(PACK):
            for cols in (halves if t == 0 else [whole]):
                difference(d1[t], t, n1_t, cols)
            nc.scalar.activation(out=d1_gained[:, t, :], in_=d1[t], func=ACT.Copy, scale=gain[:, t : t + 1])
            difference(d2[:, t, :], t, n2_t, halves[0])
        w2_lo = deal(nc.scalar.copy, w2_raw, 0, "w2_lo", 1)
        w2_hi = deal(nc.scalar.copy, w2_raw, 1, "w2_hi", 1)
        difference(d2[:, 0, :], 0, n2_t, halves[1])
        hidden(0)
        w2_q = quantize_pair(w2_lo, "w2_q01")
        quantize_hidden(0)
        for t in range(1, PACK):
            difference(d2[:, t, :], t, n2_t, halves[1])
        w2_q = w2_q + quantize_pair(w2_hi, "w2_q23")
        hidden(1)
        hidden(2)
        quantize_hidden(1)
        quantize_hidden(2)

        shared = sb("shared", [P, S + HALF], F32)
        h_sb = [st_win[0][:, right], shared[:, HALF : HALF + S], h_win[2][:, whole], h_win[3][:, whole]]
        gate = [sb("gate%d" % t, [P, S], F32) for t in range(PACK)]

        def second_layer(t, cols, b, copy):
            acc = bank(b, "h%d_%d" % (t, cols.start))[:, 0 : cols.stop - cols.start]
            product(acc, w2_q[t], z_q, cols)
            if t not in h_win:
                nc.scalar.activation(out=gate[t][:, cols], in_=acc, func=ACT.Sigmoid)
            copy(out=h_sb[t][:, cols], in_=acc)
            return acc

        second_layer(0, pieces[0], 5, nc.scalar.copy)
        second_layer(1, halves[0], 0, nc.scalar.copy)
        second_layer(0, pieces[1], 6, nc.vector.tensor_copy)
        second_layer(0, pieces[2], 7, nc.scalar.copy)
        second_layer(1, halves[1], 1, nc.scalar.copy)
        h_acc = {}
        for t in h_win:
            h_acc[t] = second_layer(t, whole, t, nc.scalar.copy)
            nc.scalar.activation(out=gate[t][:], in_=h_win[t][:].indirect(n3_t[:]), func=ACT.Sigmoid)

        st = [st_win[t][:, whole] for t in range(PACK)]
        far = [shared[:, whole], st[last], sb("far2", [P, S], F32)[:], sb("far3", [P, S], F32)[:]]
        res = [sb("res%d" % t, [P, S], F32) for t in range(PACK)]
        out_rows = out.rearrange("(p t) c -> p t c", t=PACK)

        def fetch(t, cols):
            nc.vector.tensor_copy(out=far[t][:, cols], in_=st_win[t][:].indirect(entries(n3_t, cols)))

        def larger(t, cols):
            nc.vector.tensor_tensor(out=res[t][:, cols], in0=st[t][:, cols], in1=far[t][:, cols], op=ALU.max)
            nc.sync.dma_start(out_rows[:, t, cols], res[t][:, cols])

        for t in range(2):
            for cols in halves:
                nc.vector.tensor_tensor(out=st[t][:, cols], in0=gate[t][:].indirect(entries(n3_t, cols)), in1=h_sb[t][:, cols], op=ALU.mult)
        nc.gpsimd.tensor_tensor(out=st[2], in0=h_sb[2], in1=gate[2][:], op=ALU.mult)
        fetch(0, whole)
        fetch(1, whole)
        larger(0, whole)
        larger(1, whole)
        head, tail = slice(0, S - S // 4), slice(S - S // 4, S)
        nc.gpsimd.tensor_tensor(out=st[last][:, head], in0=h_sb[last][:, head], in1=gate[last][:, head], op=ALU.mult)
        fetch(2, whole)
        nc.vector.tensor_tensor(out=st[last][:, tail], in0=h_acc[last][:, tail], in1=gate[last][:, tail], op=ALU.mult)
        larger(2, whole)
        for cols in halves:
            fetch(last, cols)
        for cols in halves:
            larger(last, cols)
